import numpy as np, ml_dtypes
CORES = [6,15,38,47]
N = 4
BF = ml_dtypes.bfloat16
def gentries(a):
    return np.ascontiguousarray(a.reshape(8, 16, -1).transpose(0, 2, 1)).reshape(8, -1)
def gtable(e):
    e = np.asarray(e); return np.ascontiguousarray(e.reshape(8, -1, 16).transpose(0, 2, 1)).reshape(128, -1).astype(np.int32)
def f(rng, *shape):
    return (rng.standard_normal(shape, dtype=np.float32) * np.exp2(rng.integers(-2, 3, shape[:-1] + (1,)))).astype(BF)
def wide(rng, *shape):
    v = f(rng, *shape).astype(np.float32); k = shape[:-2] + (1, shape[-1])
    return (v * np.exp2(rng.integers(-6, 7, k)) * (rng.random(k) > 0.0625)).astype(BF)
V, W, G, P, Q, RO = 2560, 4096, 256, 256, 64, 4
M = V + (N - 1) * G + 1
def nodes(an, of):
    A = np.full((N, 8, M), M - 1, np.int64); A[..., :V] = an
    O = np.zeros((N, 8, M), np.int64); O[..., :M - 1] = of
    return A, O
def dates(A, O):
    s, p = O, A
    for i in range(3):
        s = s + np.take_along_axis(s, p, 2); p = np.take_along_axis(p, p, 2)
    return s & (W - 1)
def parts(rng):
    u = rng.random((N, 8, V))
    an = np.where(u < 0.25, M - 1, np.where(u < 0.4, rng.integers(V, M - 1, (N, 8, V)), rng.integers(0, V, (N, 8, V))))
    return an, rng.integers(0, W, (N, 8, M - 1)), rng.integers(0, 256, (N, 8, 16, W)), rng.integers(0, V, (N, 8, (N - 1) * G))
def statures(rng):
    sc = np.exp2(rng.integers(-2, 3, (1, 8, 16, 1)).astype(np.float64)); sh = rng.choice(np.array([-0.8, -0.5, -0.2, 0.1]), (N, 8, 1, 1))
    x = rng.standard_normal((N, 8, 16, V)) + 0.7 * rng.standard_normal((N, 8, 1, V)) + sh
    s = rng.standard_normal((N, 8, 16, W)) + 0.7 * rng.standard_normal((N, 8, 1, W))
    return np.floor(8 * x) * 0.125 * sc, np.floor(8 * s) * 0.125 * sc
def pack(x, an, of, s, wk, snd):
    b = lambda v: np.ascontiguousarray(v).reshape(N, 128, -1).astype(np.float32).astype(BF)
    return {"x": b(x), "an0": np.stack([gtable(e) for e in an]), "of0": np.stack([gtable(e) for e in of]), "s0": b(s), "wk": b(wk), "snd": np.stack([gtable(e) for e in snd])}
def setup_inputs(rng):
    an, of, wk, snd = parts(rng); x, s = statures(rng)
    return pack(x, an, of, s, wk, snd)
def setup_inputs_room(rng):
    an, of, wk, snd = parts(rng); day = np.arange(W)
    an[..., 0] = M - 1; an[..., V - 1] = M - 1; of[..., 0] = 0; of[..., V - 1] = W - 2
    D = dates(*nodes(an, of))[..., :V]
    s = rng.integers(36, 61, (N, 8, 16, W)) * 0.25
    s[..., day % 4 == 3] = rng.integers(4, 29, (N, 8, 16, W // 4)) * 0.25
    o = s[1::2]; o[..., day % 4 == 1] = rng.integers(-32, -3, (o.shape[0], 8, 16, W // 4)) * 0.25
    k = rng.permutation(16)
    wk[:, :, k[0]] = 4 * rng.integers(0, 64, (N, 8, W)) + (day + 1) % 4
    wk[1::2, :, k[1]] = 4 * rng.integers(0, 64, (o.shape[0], 8, W)) + (day + 3) % 4
    x = 16 + rng.integers(0, 33, (N, 8, 16, V)) * 0.25
    for q in range(N):
        for g in range(8):
            n = int(rng.choice(np.array([0, 1, 2, P - 1, P, P + 1, P + Q]))); nf = int(rng.choice(np.array([0, 1, Q - 1, Q, Q + 1, P])))
            if q == 0: n = (P, P + 1, P - 1, 1, 0, P, P, P)[g]; nf = (Q, Q + 1, Q - 1, 1, 0, 0, P, Q + 1)[g]
            e = np.flatnonzero(D[q, g] % 2 == 0); e = e[(e > 0) & (e < V - 1)]
            w = np.concatenate([np.array([0, V - 1]), rng.permutation(e)])[:n]
            x[q, g][:, w] = rng.integers(29, 36, (16, len(w))) * 0.25
            i = w[len(w) - min(nf, len(w)):]
            x[q, g][:, i] = rng.integers(0, 4, (16, len(i))) * 0.25
    return pack(x, an, of, s, wk, snd)
def setup_inputs_ties(rng):
    an, of, wk, snd = parts(rng)
    of = rng.choice(np.array([0, 1, W - 1, W // 2, 14]), (N, 8, M - 1)); wk[:, ::2] = rng.choice(np.array([0, 1, 2, 255]), (N, 4, 16, W))
    x = np.floor(4 * rng.random((N, 8, 16, V)) * (0.3 + 0.7 * rng.random((N, 8, 1, V))))
    s = np.floor(4 * rng.random((N, 8, 16, W)) * (0.3 + 0.7 * rng.random((N, 8, 1, W)))) + 2 * (rng.random((N, 8, 1, W)) < 0.4)
    x[..., 0] = -1; x[..., V - 1] = -1
    x = np.where((x == 0) & (rng.random(x.shape) < 0.5), -0.0, x); s = np.where((s == 0) & (rng.random(s.shape) < 0.5), -0.0, s)
    return pack(x, an, of, s, wk, snd)
def setup_inputs_chains(rng):
    an, of, wk, snd = parts(rng); x, s = statures(rng); v = np.arange(V); d = int(rng.integers(0, W))
    for q in range(N):
        for g in range(8):
            k = (g + q) % 8
            if k == 0: an[q, g] = (v + 1) % V
            if k == 1: an[q, g] = v
            if k == 2: an[q, g] = rng.integers(V, M - 1, V)
            if k == 3: an[q, g] = M - 1
            if k == 4: an[q, g] = rng.choice(np.array([0, 5, V - 1]), V)
            if k == 5: an[q, g] = np.where(v == 0, M - 1, v - 1)
            if k > 5:
                an[q, g] = M - 1; of[q, g, :V] = d
                w = 1 + rng.permutation(255)[:16]; wk[q, g, :, d] = w; c = (d + 7 * w) & (W - 1)
                i = np.sort(rng.permutation(16)[:2])
                s[q, g] = 16 + 0.25 * rng.integers(0, 32, (16, W))
                s[q, g][:, c[i[0]]] = 0.25 * rng.integers(0, 16, 16)
                m = np.arange(P) if k == 6 else np.arange(int(rng.integers(0, 16)), V, 16)
                y = 28 + 0.25 * rng.integers(0, 16, (16, V))
                y[:, m] = 8 + 0.25 * rng.integers(0, 16, (16, len(m)))
                if k == 6: y[:, rng.permutation(P)[:56]] = -8 + 0.25 * rng.integers(0, 16, (16, 56))
                if k == 7: s[q, g][:, c[i[1]]] = -16 + 0.25 * rng.integers(0, 16, 16)
                x[q, g] = y
    snd[:, ::2] = rng.choice(np.array([0, 3, V // 2, V - 1]), (N, 4, (N - 1) * G))
    return pack(x, an, of, s, wk, snd)
def setup_inputs_calm(rng):
    an, of, wk, snd = parts(rng); x, s = statures(rng); q = int(rng.integers(0, N)); g = int(rng.integers(0, 8))
    x[:, g] += 64
    x[(q + 2) % N] += 64; x[q] = np.minimum(x[q], 20) - 64
    o = s[(q + 1) % N]; o[..., 1::2] -= 128
    w = rng.permutation(256)[:16]; wk[:, g, :, 0] = w; day = (7 * w) & (W - 1)
    for r in range(N):
        if r != q: s[r, g][:, day] = -2.0 ** 20
    x[q, :, :, 0] = -2.0 ** 20
    return pack(x, an, of, s, wk, snd)
def setup_inputs_spread(rng):
    an, of, wk, snd = parts(rng)
    of = np.minimum(np.exp2(13 * rng.random((N, 8, M - 1))).astype(np.int64) - 1, W - 1)
    x = np.abs(wide(rng, N, 8, 16, V).astype(np.float32)); s = np.abs(wide(rng, N, 8, 16, W).astype(np.float32))
    k = rng.permutation(8); sc = np.ones((1, 8, 1, 1), np.float32); sc[:, k[0]] = 2.0 ** -40; sc[:, k[1]] = 512
    x = np.minimum(x * sc, np.float32(2.0 ** 20)); s = np.minimum(s * sc, np.float32(2.0 ** 20))
    x[:, k[1], :, V - 1] = 2.0 ** 20; s[:, k[1], :, W - 1] = 2.0 ** 20
    return pack(x, an, of, s, wk, snd)
def check_inputs(d):
    bad = []
    for k, lo, hi in (("x", -2 ** 20, 2 ** 20), ("s0", -2 ** 20, 2 ** 20), ("wk", 0, 255), ("an0", 0, M - 1), ("of0", 0, W - 1), ("snd", 0, V - 1)):
        v = np.asarray(d[k]).astype(np.float64)
        if not (np.min(v) >= lo and np.max(v) <= hi): bad.append("range of " + k)
        elif k == "wk" and np.any(v != np.floor(v)): bad.append("whole numbers of wk")
        elif k in ("x", "s0") and np.any((v != 0) & (np.abs(v) < 2.0 ** -100)): bad.append("tiny numbers of " + k)
    return bad
def best(S, K, x, D):
    c = (D + 7 * K[:, D]) & (W - 1)
    e = np.sum((x[:, None, :] > S[:, c]).astype(np.int64), axis=0)
    k = np.argmax(e, axis=0); i = np.arange(len(D))
    return c[k, i], e[k, i]
def put(S, c, x):
    u, i = np.unique(c, return_index=True)
    S[:, u] = x[:, i]
def reference(x, an0, of0, s0, wk, snd):
    X = x.astype(np.float32).reshape(N, 8, 16, V); S = s0.astype(np.float32).reshape(N, 8, 16, W).copy(); K = wk.astype(np.float32).astype(np.int64).reshape(N, 8, 16, W)
    A, O = nodes(np.stack([gentries(e) for e in an0]).astype(np.int64), np.stack([gentries(e) for e in of0]).astype(np.int64))
    sl = np.stack([gentries(e) for e in snd]).astype(np.int64).reshape(N, 8, N - 1, G)
    odd = np.zeros(N, np.int64)
    for t in range(RO):
        D = dates(A, O)[..., :V]
        a = np.sum((X >= np.take_along_axis(S, D[:, :, None, :], 3)).astype(np.int64), axis=2)
        moves = np.zeros(N, np.int64); go = {}
        for q in range(N):
            for g in range(8):
                v = np.flatnonzero(a[q, g] < 5)[:P]
                c, e = best(S[q, g], K[q, g], X[q, g][:, v], D[q, g, v])
                ok = e >= 9 + odd[q]; w = v[ok]
                A[q, g, w] = M - 1; O[q, g, w] = c[ok]
                put(S[q, g], c[ok], X[q, g][:, w])
                moves[q] += len(w)
                r = v[~ok][:Q]; go[q, g] = (X[q, g][:, r], D[q, g, r])
        for q in range(N):
            for g in range(8):
                y, b = go[(q - 1 - t % (N - 1)) % N, g]
                c, e = best(S[q, g], K[q, g], y, b)
                ok = e >= 9 + odd[q]
                put(S[q, g], c[ok], y[:, ok])
        odd = moves & 1
        for q in range(N):
            for d in range(1, N):
                p = (q - d) % N
                O[q, :, V + (d - 1) * G:V + d * G] = np.take_along_axis(D[p], sl[p, :, d - 1], 1)
    return {"ys": S.reshape(N, 128, W).astype(BF), "yan": A[..., :V].astype(np.float32), "yof": O[..., :V].astype(np.float32)}

from concourse.bass import DstId, RemoteDMATransfer
from concourse.mybir import AluOpType as O, AxisListType, ActivationFunctionType as F

RO = 4
NE = 6672
SCRATCH, PACK = {}, {}
FILL = {"float32": 0, "bfloat16": 0, "int32": 0, "uint16": 0}
OWN = "AN WK X S OF SNDI WP OFb ANb AN0b E E1 E2 B OUT ONE B16 R2 CR".split()


def _b(names, cols, d="float32", w="sbuf"):
    for n in names.split():
        if w == "psum" or isinstance(cols, list) or n in OWN or n[:2] in ("GS", "GR"):
            SCRATCH[n] = (w, [128] + (cols if isinstance(cols, list) else [cols]), d)
        else:
            PACK[n] = ("pk_" + d, FILL[d], cols)
            FILL[d] += (cols + 15) // 16 * 16
            SCRATCH["pk_" + d] = ("sbuf", [128, FILL[d]], d)


_b("K0 K1 K2 K3 K4 K5 K6 K7", 512, "float32", "psum")
_b("CNT FD FF FP FV HC PFX", 2048, "bfloat16")
_b("ONE B16 ID LT MB I16 IM1 IM1K B32 B40 B4 BW ZER I7 IM2K CR YW YT M16b", 128, "bfloat16")
_b("M16 B16f ONEf A00 A01 A10 A11", 128)
_b("E", NE + 256, "bfloat16")
_b("E1 E2", NE, "bfloat16")
_b("E3 CMP B", 2560, "bfloat16")
_b("WP", 3344, "bfloat16")
_b("X", 2576, "bfloat16")
_b("S", 4368, "bfloat16")
_b("WK XE CM", 4096, "bfloat16")
_b("CT", 4112)
_b("EQ", 2176, "bfloat16")
_b("GT", 1024, "bfloat16")
_b("N1b C1 C2 EQS DGH DGL XS EV Q WIN", 256, "bfloat16")
_b("N1f MASK MD THP M256 CS COMB TR U RX", 256)
_b("IC ON160 P2F P4F ISG R720 W1 DLT FPm RK1", 160)
_b("CO DGf", 64)
_b("DM10 TH TMPc T10 W2 RED VF NT NTL NLE G64 E1t PE_ T1 VA LS LS2 PS RR BAD RM GP INV HS TG Lg", 16)
_b("INC RKM", 176)
_b("TT Lf", 48)
_b("GX", 24)
_b("CSg CBg TRg Ug RXg", 64)
_b("RI YI BI MI CI HI", 16, "int32")
_b("AN LOI HII N1I PLI T4I P2I P4I DI DI2 DI3", 160, "int32")
_b("OF", 208, "int32")
_b("OFd", 624, "int32")
_b("ANd AN0d", 480, "int32")
_b("SNDI DQ", 48, "int32")
_b("OFb", 624, "bfloat16")
_b("ANb AN0b", 480, "bfloat16")
_b("N1H P2H P2B P4H P4B BT", 160, "bfloat16")
_b("R2 SG0 SG1", 512, "bfloat16")
_b("DH DLO", 176, "bfloat16")
_b("B16v C16v RFB", 16, "bfloat16")
_b("NG", 320, "bfloat16")
_b("HALF GH GLo WINg", 64, "bfloat16")
_b("GD", 768, "bfloat16")
_b("XGE CMg", 1024, "bfloat16")
_b("EQg", 160, "bfloat16")
_b("IDL PL P1L P2L P4L DL", 160, "uint16")
_b("BL CL DNL VL REP POSE POSS POSG NL DGN POSQ", 16, "uint16")
_b("SL CgL CRUg", 64, "uint16")
_b("CAN CRU", 256, "uint16")
_b("GI3", [3, 16], "int32")
_b("DI4", [3, 3, 16], "int32")
_b("OUT", 2560)
for _t in range(RO):
    _b("GM%d LAND%d" % (_t, _t), [3, 3, 16], "bfloat16")
    _b("GS%d GR%d" % (_t, _t), 72, "bfloat16")

SEMAPHORES = ["cv", "cs", "cp", "cg"] + ["d%d" % k for k in range(90)] + \
    ["%s%d" % (k, t) for k in ("ga", "gl", "ua", "ul") for t in range(RO)]


def rank_program(g, core, T, topo):
    rank = T.rank_of(core)
    if rank is None:
        return
    N = len(T.cores)
    V, S, P, G = g.vector, g.scalar, g.tensor, g
    QU = {"v": V, "s": S, "p": P, "g": G, "y": g.sync}
    cnt = {"cv": 0, "cs": 0, "cp": 0, "cg": 0}
    known = {q: {} for q in QU}
    acc, bank, nd = {}, {}, [0]

    def r(name, lo=0, hi=None, step=1, part=None):
        ph, o, w = PACK.get(name, (name, 0, None))
        if hi is None:
            hi = w or T[name].shape[1]
        ap = T[ph][:, o + lo:o + hi:step] if step > 1 else T[ph][:, o + lo:o + hi]
        return (ap, name, lo, hi, step, lo % step, part)

    def rp(name, row, lo, hi):
        return (T[name][row::16, lo:hi], name, lo, hi, 1, 0, row)

    def whole(name, ap=None, part=None):
        return (T[name][:] if ap is None else ap, name, 0, 1 << 30, 1, 0, part)

    def ind(win, off):
        return (win[0].indirect(off[0]), [win, off])

    def col(c):
        return r("CO", c, c + 1)

    def flat(x):
        if x is None or isinstance(x, (int, float)):
            return []
        return list(x[1]) if isinstance(x[1], list) else [x]

    def lap(a, b):
        if a[1] <= b[0] or b[1] <= a[0] or (a[2] > 1 and a[2] == b[2] and a[3] != b[3]):
            return False
        return a[4] is None or b[4] is None or a[4] == b[4]

    def need(q, evs):
        for e in sorted(evs, key=lambda e: -sum(e[2].values())):
            if known[q].get(e[0], 0) >= e[1]:
                continue
            QU[q].wait_ge(T.sem[e[0]], e[1])
            for k, v in list(e[2].items()) + [(e[0], e[1])]:
                if known[q].get(k, 0) < v:
                    known[q][k] = v

    def op(q, call, reads, writes, dma=None):
        deps = {}

        def dep(e):
            if e[0] not in deps or deps[e[0]][1] < e[1]:
                deps[e[0]] = e
        tag = q if dma is None else "dma"
        both = [(x, 0) for x in reads] + [(x, 1) for x in writes]
        for R, isw in both:
            if R[1][0] == "K":
                for qq, e in bank.get(R[1], {}).items():
                    if qq != q:
                        dep(e)
                continue
            for a in acc.get(R[1], []):
                if (isw or a[1]) and lap(a[0], R[2:7]):
                    dep(a[3])
        if q == "g" and dma is None and cnt["cg"]:
            dep(("cg", cnt["cg"], {}))
        need(q, list(deps.values()))
        inst = call()
        if dma is None:
            c, n = "c" + q, cnt["c" + q] + 1
            inst.then_inc(T.sem[c], 1)
        elif dma == "local":
            c, n = "d%d" % nd[0], 16
            nd[0] += 1
            inst.then_inc(T.sem[c], 16)
        else:
            c, n = dma
        cnt[c] = n
        ev = (c, n, dict(known[q]))
        for R, isw in both:
            if R[1][0] == "K":
                bank.setdefault(R[1], {})[q] = ev
                continue
            reg = R[2:7]
            L = acc.get(R[1], [])
            if isw and reg[2] == 1 and reg[4] is None:
                L = [a for a in L if not (reg[0] <= a[0][0] and a[0][1] <= reg[1])]
            elif not isw:
                L = [a for a in L if a[1] or a[2] != tag or tag == "dma" or a[0] != reg]
            L.append((reg, isw, tag, ev))
            acc[R[1]] = L

    def arrive(R, sem, n):
        cnt[sem] = n
        acc.setdefault(R[1], []).append((R[2:7], 1, "dma", (sem, n, {})))

    def ap(x):
        return x if x is None or isinstance(x, (int, float)) else x[0]

    def tt(o, a, b, f):
        op("v", lambda: V.tensor_tensor(o[0], a[0], b[0], f), flat(a) + flat(b), flat(o))

    def ts(o, a, s1, s2, f, f2=None):
        more = () if f2 is None else (f2,)
        op("v", lambda: V.tensor_scalar(o[0], a[0], ap(s1), ap(s2), f, *more), flat(a) + flat(s1) + flat(s2), flat(o))

    def cp(o, a):
        op("v", lambda: V.tensor_copy(o[0], a[0]), flat(a), flat(o))

    def ms(o, v, apx=None):
        op("v", lambda: V.memset(o[0] if apx is None else apx, v), [], flat(o))

    def tr(o, a):
        op("v", lambda: V.transpose(o[0], a[0]), flat(a), flat(o))

    def scan(o, d0, d1, init, f0, f1):
        op("v", lambda: V.tensor_tensor_scan(o[0], d0[0], d1[0], init, f0, f1), flat(d0) + flat(d1), flat(o))

    def red(o, a):
        op("v", lambda: V.tensor_reduce(o[0], a[0], AxisListType.X, O.add), flat(a), flat(o))

    def act(o, a, f=F.Copy, bias=None, scale=None):
        kw = {}
        if bias is not None:
            kw["bias"] = ap(bias)
        if scale is not None:
            kw["scale"] = ap(scale)
        op("s", lambda: S.activation(o[0], a[0], f, **kw), flat(a) + flat(bias) + flat(scale), flat(o))

    def mm(o, pairs, start=True, stop=True):
        def call():
            i = None
            for k, (l, x) in enumerate(pairs):
                i = P.matmul(o[0], l[0], x[0], start and k == 0, stop and k == len(pairs) - 1)
            return i
        op("p", call, [z for l, x in pairs for z in (l, x)], [o])

    def fam(f, src, c0, c1):
        return [(r(f, 128 * i, 128 * i + 128), r(src, 16 * c0 + i, 16 * c1, 16)) for i in range(16)]

    def conv(f, src, c0, c1, o, extra=()):
        mm(o, list(extra) + fam(f, src, c0, c1))

    def dma(q, o, a):
        op(q, lambda: QU[q].dma_start(o[0], a[0]), [a], [o], "local")

    def iota(o, pat, base=0, cm=0, apx=None):
        kw = {} if o[1] == "PI32" else {"allow_small_or_imprecise_dtypes": True}
        op("g", lambda: G.iota(o[0] if apx is None else apx, pat, base, cm, **kw), [], [o])

    def gsel(o, a, pat, base, cm):
        op("g", lambda: G.affine_select(o[0], a[0], pat, O.is_ge, 0.0, base, cm), [a], [o])

    def sel(dst, items):
        for k, (row, val) in enumerate(items):
            ts(col(dst) if k == 0 else col(40 + k), col(0), float(row), float(val), O.is_equal, O.mult)
        for k in range(1, len(items)):
            tt(col(dst), col(dst), col(40 + k), O.add)

    dma("y", r("OF"), whole("of0"))
    dma("s", r("AN"), whole("an0"))
    dma("y", r("WK"), whole("wk"))
    dma("s", r("SNDI"), whole("snd"))
    dma("y", r("X", 0, 2560), whole("x"))
    dma("s", r("S", 0, 4096), whole("s0"))
    def pidx(n):
        o = PACK["RI"][1]
        return (T["pk_int32"][:, o:o + n], "PI32", 0, n, 1, 0, None)
    iota(pidx(2), [[0, 2]], 0, 1)
    ms(r("ONE"), 1.0)
    iota(r("M16"), [[0, 8], [1, 16]])
    gsel(r("B16"), r("ONE"), [[-16, 8], [0, 16]], 0, 1)
    gsel(r("B16"), r("B16"), [[16, 8], [0, 16]], 15, -1)
    iota(r("WP", 0, 2560), [[0, 2560]])
    iota(r("IC"), [[1, 160]])
    iota(r("R2", part="lo"), [[1, 32], [0, 16]], apx=T.R2[0:64, :])
    iota(r("R2", part="hi"), [[0, 32], [1, 16]], apx=T.R2[64:128, :])
    iota(r("M256"), [[0, 16], [1, 16]])
    iota(r("N1f"), [[1, 256]], 1)
    iota(r("NT"), [[32, 8], [0, 2]], 4096)
    iota(r("NTL"), [[16, 16]], 4096)
    iota(r("T10"), [[1, 16]])
    iota(r("E", 3344, NE), [[0, NE - 3344]])
    ts(r("YI", 0, 1), pidx(1), 31, None, O.bitwise_and)
    ts(r("YI", 1, 2), pidx(1), 15, None, O.bitwise_and)
    cp(col(0), r("YI", 1, 2))
    cp(col(1), r("YI", 0, 1))
    ms(r("WP", 2560, 3344), 0.0)
    sel(7, [(6, 13)])
    ts(r("WP", 2560, 3344), r("WP", 2560, 3344), col(7), None, O.add)
    ms(r("CNT"), 0.0)
    ts(r("LOI"), r("AN"), 15, None, O.bitwise_and)
    ts(r("HII"), r("AN"), 4, None, O.arith_shift_right)
    for k in range(2):
        ts(r("OFd", 208 * k, 208 * k + 208), r("OF"), 4 * k, 15, O.arith_shift_right, O.bitwise_and)
    ts(r("OFd", 416, 624), r("OF"), 8, None, O.arith_shift_right)
    ts(r("W1"), r("LOI"), 48, 2400, O.mult, O.add)
    ts(r("R720"), r("HII"), 208, 720, O.is_ge, O.mult)
    cp(r("OFb"), r("OFd"))
    tt(r("W1"), r("W1"), r("HII"), O.add)
    ts(r("ISG"), r("HII"), 160, None, O.is_ge)
    ts(r("AN0d", 0, 160), r("AN"), 15, None, O.bitwise_and)
    tt(r("W1"), r("W1"), r("R720"), O.add)
    ts(r("AN0d", 160, 320), r("AN"), 4, 15, O.arith_shift_right, O.bitwise_and)
    tt(r("DLT"), r("W1"), r("AN"), O.subtract)
    ts(r("AN0d", 320, 480), r("AN"), 8, None, O.arith_shift_right)
    tt(r("DLT"), r("DLT"), r("ISG"), O.mult)
    cp(r("AN0b"), r("AN0d"))
    tt(r("N1I"), r("DLT"), r("AN"), O.add)
    ts(r("FPm"), r("LOI"), 160, None, O.mult)
    ts(r("ANd", 0, 160), r("N1I"), 15, None, O.bitwise_and)
    ts(r("ANd", 160, 320), r("N1I"), 4, 15, O.arith_shift_right, O.bitwise_and)
    ts(r("ANd", 320, 480), r("N1I"), 8, None, O.arith_shift_right)
    tt(r("FPm"), r("FPm"), r("HII"), O.add)
    cp(r("ANb"), r("ANd"))
    for k in range(3):
        dma("ysy"[k], rp("WP", k, 0, 2560), r("OFb", 208 * k, 208 * k + 160))
        dma("sys"[k], rp("WP", k, 2560, 3328), r("OFb", 208 * k + 160, 208 * k + 208))
        dma("ysy"[k], rp("WP", 8 + k, 0, 2560), r("AN0b", 160 * k, 160 * k + 160))
        dma("sys"[k], rp("WP", 4 + k, 0, 2560), r("ANb", 160 * k, 160 * k + 160))
    tt(r("DLT"), r("W1"), r("FPm"), O.subtract)
    ts(col(13), col(0), 160.0, None, O.mult)
    tt(r("DLT"), r("DLT"), r("ISG"), O.mult)
    ts(r("IDL"), r("IC"), col(13), None, O.add)
    tt(r("PLI"), r("DLT"), r("FPm"), O.add)
    ts(col(8), col(0), 3.5, None, O.is_lt)
    ts(col(9), col(0), 6.5, None, O.is_gt)
    cp(r("PL"), r("PLI"))
    tt(col(8), col(8), col(9), O.add)
    for q in range(8):
        cp(r("CNT", 16 * q, 2048, 129), r("B16", 16 * q, 16 * q + 16))
    sel(5, [(4, 1), (5, 16), (6, 256)])
    act(r("E1", 2560, 3344), r("WP", 2560, 3344))

    def consts(j):
        if j == 0:
            ts(r("FP"), r("CNT"), col(5), None, O.mult)
            ts(r("M16b"), r("M16"), col(0), None, O.is_equal)
            tt(r("ID"), r("M16b"), r("B16"), O.mult)
            ts(r("I7"), r("ID"), 7.0, None, O.mult)
            ts(r("IM2K"), r("ID"), -2048.0, None, O.mult)
            ms(r("CR", part="lo"), 0.25, T.CR[0:64, :])
            ms(r("CR", part="hi"), 1.0 / 64, T.CR[64:128, :])
            for b in range(8):
                ms(col(48 + b), 512.0 * b - 4095.5)
                ms(col(56 + b), 512.0 * b - 2048.0)
        if j == 1:
            sel(4, [(0, 1), (1, 16), (2, 256)])
            ts(r("FD"), r("CNT"), col(4), None, O.mult)
            ts(r("IM1"), r("ID"), -1.0, None, O.mult)
            ts(r("HC"), r("CNT"), 0.5, None, O.mult)
            ms(r("HALF"), 0.5)
            ms(col(30), 2.0 ** -112)
            ms(col(31), -2.0 ** -112)
            ts(r("MB"), r("M16"), col(0), None, O.is_gt)
            tt(r("LT"), r("MB"), r("B16"), O.mult)
            ts(r("MB"), r("M16"), 1.0, None, O.add)
            tt(r("MB"), r("MB"), r("B16"), O.mult)
            ms(r("ON160"), 1.0)
            ms(r("INC", 0, 1), 1.0)
            ms(r("RKM", 160, 176), 0.0)
            ms(r("W2", 10, 16), 1e6)
            ms(r("DH", 160, 176), 0.0)
            ms(r("DLO", 160, 176), 0.0)
            ms(r("X", 2560, 2576), 0.0)
            ms(r("CT", 4096, 4112), -4194304.0)
            cp(r("SL", 0, 48), r("SNDI"))
            for i in range(16):
                ts(r("PFX", 128 * i, 128 * i + 128), r("MB"), float(i + 1), None, O.is_ge)
        if j == 2:
            ts(r("N1b"), r("N1f"), 1.0, None, O.mult)
            ts(r("FV"), r("CNT"), col(0), None, O.mult)
            ts(col(10), col(0), 9.5, None, O.is_lt)
            ts(r("DM10"), r("T10"), col(0), None, O.is_equal)
            ts(r("B32"), r("B16"), 32.0, None, O.mult)
            ts(r("B40"), r("B16"), 40.0, None, O.mult)
            ts(col(9), col(0), -0.0625, 0.9375, O.mult, O.add)
            ts(r("MASK"), r("M256"), 0.5, None, O.is_gt)
            ts(r("NT"), r("NT"), col(1), None, O.add)
            ts(r("NTL"), r("NTL"), col(0), None, O.add)
            ts(r("NLE"), r("NTL"), float(NE - 4096), None, O.add)
            ts(r("G64"), r("NTL"), -4032.0, None, O.add)
            ms(r("TH", 0, 1), 41.0)
            ms(r("TH", 1, 2), 9.0)
            ts(r("MD"), r("M256"), col(0), None, O.is_equal)
            cp(r("REP"), r("T10"))
            cp(r("B16f"), r("B16"))
        if j == 3:
            ts(col(2), col(1), 15.5, None, O.is_gt)
            ts(col(3), col(1), 15.5, None, O.is_lt)
            ms(r("A01", 0, 16), 0.0)
            ms(r("A10", 112, 128), 0.0)
            ts(r("A00"), r("ID"), col(3), None, O.mult)
            ts(r("A01", 16, 128), r("ID", 0, 112), col(3), None, O.mult)
            ts(r("A10", 0, 112), r("ID", 16, 128), col(2), None, O.mult)
            ts(r("A11"), r("ID"), col(2), None, O.mult)
            tt(r("RX"), r("M256"), r("M256"), O.mult)
            ts(r("TR"), r("RX"), 9.0, 128.0, O.is_equal, O.mult)
            ts(r("RX"), r("RX"), 100.0, 13.0, O.is_equal, O.mult)
            tt(r("Q"), r("TR"), r("RX"), O.add)
            ts(r("IM1K"), r("ID"), -1024.0, None, O.mult)
            ts(r("I16"), r("ID"), 16.0, None, O.mult)
            sel(6, [(3, 26)])
            ts(r("FF"), r("CNT"), col(6), None, O.mult)
        if j == 4:
            act(r("E", 2560, 3344), r("WP", 2560, 3344))
            dma("y", r("E1", 3344, NE), r("E", 3344, NE))
            dma("y", r("E2", 3344, NE), r("E", 3344, NE))
            for k in range(4):
                ts(r("BI", 0, 1), r("YI", 1, 2), k, 1, O.arith_shift_right, O.bitwise_and)
                ts(col(20 + k), r("BI", 0, 1), 2.0 ** -(1 << k) - 1.0, 1.0, O.mult, O.add)
            tt(col(20), col(20), col(21), O.mult)
            tt(col(22), col(22), col(23), O.mult)
            tt(col(20), col(20), col(22), O.mult)
            ts(r("BW"), r("B16"), col(20), None, O.mult)
            ts(r("B4"), r("B16"), 4.0, None, O.mult)
            ms(r("ZER"), 0.0)
            for i in range(16):
                ms(r("THP", i, 256, 16), 2.0 ** (1 - i))
            ms(r("ONEf"), 1.0)
            ts(r("T4I"), r("N1I"), 4, None, O.arith_shift_right)
            cp(r("N1H"), r("T4I"))
            for h, l, f, i in (("P2H", "P2B", "P2F", "P2I"), ("P4H", "P4B", "P4F", "P4I")):
                cp(r(i), r(f))
                ts(r("DI3"), r(i), 4, None, O.arith_shift_right)
                cp(r(h), r("DI3"))
                ts(r("DI3"), r(i), 15, None, O.bitwise_and)
                cp(r(l), r("DI3"))

    def ctab(b):
        K, sg = ("K4", "K5")[b % 2], "SG%d" % (b % 2)
        tv = [(r("I7"), r("WK", 512 * b, 512 * b + 512)), (r("CR"), r("R2"))]
        mm(r(K), tv)
        act(r(sg), r(K), F.Sign, bias=col(48 + b))
        mm(r(K), tv + [(r("IM2K"), r(sg))])
        act(r("CT", 512 * b, 512 * b + 512), r(K), F.Identity, bias=col(56 + b))

    VC = [(32, 96), (96, 160)]

    def addend(name, c0, c1):
        dma("y", r("B", 16 * c0, 16 * c1), r(name, 16 * c0, 16 * c1))

    def level(win, lst, out, f, extra, fill=None):
        W = r(win, 0, NE)

        def cv(c0, c1):
            conv(f, out, c0, c1, r("K0", c0, c1), [(r(l), r(x, c0, c1)) for l, x in extra])

        def vec(c0, c1):
            tt(r(out, 16 * c0, 16 * c1), ind(W, r(lst, c0, c1)), r("B", 16 * c0, 16 * c1), O.add)
            if out != "E3":
                addend(out, c0, c1)
        act(r("GT", 0, 512), ind(W, r(lst, 0, 32)))
        vec(*VC[0])
        mm(r("K1"), [(r("ID"), r("GT", 0, 512)), (r("ID"), r(win, 0, 512))])
        act(r(out, 0, 512), r("K1"))
        cv(*VC[0])
        if fill:
            fill()
        vec(*VC[1])
        cv(0, 32)
        cv(*VC[1])

    def ttol(src, n, K, k0):
        for m2, (a0, a1) in enumerate((("A00", "A01"), ("A10", "A11"))):
            mm(r(K, k0 + m2, k0 + n, 2), [(r(a0), r(src, 0, n, 2)), (r(a1), r(src, 1, n, 2))])

    def dd1(L, n, RXn):
        tt(r(RXn, 0, n), ind(r(L, 0, n // 16), r("REP", 0, n // 16)), r("MD", 0, n), O.mult)
        mm(r("K5", 0, n), [(r("B16f"), r(RXn, 0, n))])

    def dd2(L, n, CRn, EQn):
        cp(r(CRn, 0, n), r("K5", 0, n))
        z = [(r("ZER"), r("N1b", 0, n))]
        mm(r("K5", 256, 256 + n), z, stop=False)
        o = 0
        for m in range(n // 16):
            w = n - 16 * m
            ts(r(EQn, o, o + w), r(CRn, 16 * m, n), r(L, m, m + 1), None, O.is_equal)
            mm(r("K5", 256 + 16 * m, 272 + 16 * m), [(r("BW"), r(EQn, o, o + 16))], start=False, stop=False)
            if w > 16:
                mm(r("K5", 272 + 16 * m, 256 + n), [(r("B4"), r(EQn, o + 16, o + w))], start=False, stop=False)
            o += w
        mm(r("K5", 256, 256 + n), z, start=False)

    def dd3(n, WINn):
        tt(r(WINn, 0, n), r("K5", 256, 256 + n), r("THP", 0, n), O.is_lt)
        conv("CNT", WINn, 0, n // 16, r("K3", 48, 48 + n // 16))

    def dd4(L, n, posn, xs):
        k = n // 16
        ts(r("LS", 0, k), r("K3", 48, 48 + k), 8.0, None, O.is_lt)
        tt(r("LS2", 0, k), r("LS", 0, k), r("NTL", 0, k), O.mult)
        tt(r("PS", 0, k), r("LS2", 0, k), r(L, 0, k), O.max)
        cp(r(posn, 0, k), r("PS", 0, k))
        cp(ind(r("S"), r(posn, 0, k)), xs)

    def guest1(t):
        gr = "GR%d" % t
        arrive(r(gr), "ua%d" % t, 8)
        tt(r("DGf", 0, 4), r(gr, 64, 68), r(gr, 68, 72), O.add)
        cp(r("DGN", 0, 4), r("DGf", 0, 4))
        cp(r("CgL"), ind(r("CT"), r("DGN", 0, 4)))
        for k in range(16):
            if k % 3 == 2:
                act(r("XGE", k, 1024, 16), r(gr, 0, 64))
            else:
                cp(r("XGE", k, 1024, 16), r(gr, 0, 64))
        act(r("CSg"), ind(r("CT"), r("DGN", 0, 4)), F.Identity, bias=col(9), scale=2.0 ** -16)

    def guest2(t):
        tt(r("CMg"), ind(r("S", 0, 4096), r("CgL")), r("XGE"), O.is_lt)
        conv("CNT", "CMg", 0, 64, r("K4", 256, 320))

    def guest3(t):
        tt(r("CBg"), r("K4", 256, 320), r("CSg"), O.add)
        tr(r("TRg"), r("CBg"))
        scan(r("Ug"), r("MASK", 0, 64), r("TRg"), 0.0, O.mult, O.max)
        M = r("Ug", 15, 64, 16)
        ts(r("MI", 0, 4), M, 65536.0, None, O.mult)
        ts(r("T1", 0, 4), M, r("TH", 2 * t + 1, 2 * t + 2), None, O.is_lt)
        ts(r("CI", 0, 4), r("MI", 0, 4), 4095, None, O.bitwise_and)
        tt(r("VA", 0, 4), r("T1", 0, 4), r("NT", 0, 4), O.mult)
        tt(r("TG", 0, 4), r("VA", 0, 4), r("CI", 0, 4), O.max)
        ttol("TG", 4, "K6", 112)

    def guest4(t):
        cp(r("Lg", 0, 4), r("K6", 112, 116))
        dd1("Lg", 64, "RXg")

    CH = ((0, 64), (64, 128), (128, 160))
    for t in range(RO):
        more = t < RO - 1
        if t == 0:
            for c0, c1 in CH:
                act(r("E", 16 * c0, 16 * c1), ind(r("WP"), r("IDL", c0, c1)), F.Identity, scale=col(8))
                tt(r("E1", 16 * c0, 16 * c1), ind(r("WP"), r("PL", c0, c1)), r("E", 16 * c0, 16 * c1), O.add)
                addend("E1", c0, c1)
            act(r("E2", 2560, 3344), r("WP", 2560, 3344))
            consts(0)
            for c0, c1 in CH:
                conv("FP", "E1", c0, c1, r("K0", c0, c1))
            ctab(0)
            ctab(1)
            cp(r("P2L"), r("K0", 0, 160))
            cp(r("P2F"), r("K0", 0, 160))
            for win, lst, out, f in (("E1", "P2L", "E2", "FP"), ("E2", "P4L", "E3", "FD")):
                for c0, c1 in CH:
                    tt(r(out, 16 * c0, 16 * c1), ind(r(win, 0, 3344), r(lst, c0, c1)), r("B", 16 * c0, 16 * c1), O.add)
                    if out == "E2":
                        addend("E2", c0, c1)
                    elif c0 == 0:
                        ctab(4)
                        ctab(5)
                    conv(f, out, c0, c1, r("K0", c0, c1))
                if out == "E2":
                    ctab(2)
                    ctab(3)
                    consts(1)
                    tt(r("P4F"), r("K0", 0, 160), r("P2F"), O.subtract)
                    cp(r("P4L"), r("P4F"))
            consts(2)
        else:
            level("E", "P1L", "E1", "FF", [("I16", "P2H"), ("ID", "P2B")])
            dd4("Lf", 256, "POSS", r("XS"))
            guest1(t - 1)
            cp(r("P2L"), r("K0", 0, 160))
            level("E1", "P2L", "E2", "FF", [("I16", "P4H"), ("ID", "P4B")])
            guest2(t - 1)
            cp(r("P4L"), r("K0", 0, 160))
            level("E2", "P4L", "E3", "FD", [], lambda: guest3(t - 1))
            guest4(t - 1)
        cp(r("DI"), r("K0", 0, 160))
        ts(r("DI"), r("DI"), 4095, None, O.bitwise_and)
        if t:
            dd2("Lg", 64, "CRUg", "EQg")
        cp(r("DL"), r("DI"))
        ts(r("DI2"), r("DI"), 4080, None, O.bitwise_and)
        ts(r("DI3"), r("DI"), 15, None, O.bitwise_and)
        if t:
            dd3(64, "WINg")
        cp(r("DH", 0, 160), r("DI2"))
        cp(r("DLO", 0, 160), r("DI3"))
        if t:
            dd4("Lg", 64, "POSQ", r("GR%d" % (t - 1), 0, 64))
        else:
            ctab(6)
        W = r("S", 0, 4096)
        act(r("GT", 0, 512), ind(W, r("DL", 0, 32)))
        for j, (c0, c1) in enumerate(VC):
            tt(r("CMP", 16 * c0, 16 * c1), ind(W, r("DL", c0, c1)), r("X", 16 * c0, 16 * c1), O.is_le)
            if j == 0:
                mm(r("K2"), [(r("ID"), r("X", 0, 512)), (r("IM1"), r("GT", 0, 512))])
                act(r("CMP", 0, 512), r("K2"), F.Sign, bias=col(30))
            else:
                conv("HC", "CMP", 0, 32, r("K1", 0, 32), [(r("B16"), r("HALF", 0, 32))])
            conv("CNT", "CMP", c0, c1, r("K1", c0, c1))
        if more:
            act(r("GD"), ind(r("E3"), r("SL", 0, 48)))
        if t == 0:
            ctab(7)
            consts(3)
        ts(r("BT"), r("K1", 0, 160), 4.5, None, O.is_lt)
        mm(r("K0", 160, 320), [(r("B16"), r("BT"))])
        mm(r("K2", 0, 160), [(r("LT"), r("BT"))])
        mm(r("K2", 320, 330), [(r("PFX", 128 * i, 128 * i + 128), r("BT", i, 160, 16)) for i in range(16)])
        scan(r("INC", 1, 161), r("ON160"), r("K0", 160, 320), 1.0, O.mult, O.add)
        tt(r("TMPc", 0, 10), r("INC", 16, 161, 16), r("DM10", 0, 10), O.mult)
        red(r("RED", 0, 1), r("TMPc", 0, 10))
        ts(r("C1"), r("N1b"), r("RED", 0, 1), col(10), O.is_ge, O.mult)
        conv("CNT", "C1", 0, 16, r("K3", 0, 16))
        if more:
            conv("FD", "GD", 0, 48, r("K7", 64, 112))
        tt(r("W2", 0, 10), r("K2", 320, 330), r("INC", 0, 160, 16), O.add)
        tt(r("RK1"), r("K2", 0, 160), r("INC", 0, 160), O.add)
        tt(r("RKM", 0, 160), r("RK1"), r("BT"), O.mult)
        cp(r("BL"), r("K3", 0, 16))
        ts(r("B16v"), r("K3", 0, 16), 16.0, None, O.mult)
        tt(r("C2"), ind(r("W2"), r("BL")), r("N1f"), O.is_le)
        conv("CNT", "C2", 0, 16, r("K3", 16, 32), [(r("ID"), r("B16v"))])
        if more:
            for d in range(3):
                cp(whole("GI3", T.GI3[:, d, :]), r("K7", 64 + 16 * d, 80 + 16 * d))
            for k in range(3):
                ts(whole("DI4", T.DI4[:, :, k, :], k), whole("GI3"), 4 * k, 15, O.arith_shift_right, O.bitwise_and)
        cp(r("CL"), r("K3", 16, 32))
        ts(r("C16v"), r("K3", 16, 32), 16.0, None, O.mult)
        tt(r("EQS"), ind(r("RKM"), r("CL")), r("N1f"), O.is_equal)
        conv("FV", "EQS", 0, 16, r("K3", 32, 48), [(r("ID"), r("C16v"))])
        tt(r("DGH"), ind(r("DH"), r("CL")), r("EQS"), O.mult)
        tt(r("DGL"), ind(r("DLO"), r("CL")), r("EQS"), O.mult)
        conv("CNT", "DGL", 0, 16, r("K6", 0, 16), fam("CNT", "DGH", 0, 16))
        cp(r("VL"), r("K3", 32, 48))
        cp(r("XS"), ind(r("X"), r("VL")))
        for k in (0, 4, 8, 12):
            act(r("XE", k, 4096, 16), r("XS"))
        for k in (1, 5, 9):
            gsel(r("XE", k, 4096, 16), r("XS"), [[0, 256]], 1, 0)
        if more:
            gm, ld = "GM%d" % t, "LAND%d" % t
            cp(whole(gm), whole("DI4"))
            tl = []
            for d in range(1, N):
                dst = T.cores[(rank + d) % N]
                rid, pid, _ = topo.addr(dst)
                e = topo.engines(core, dst)
                tl.append(RemoteDMATransfer(src=T[gm][:, d - 1], dst=T[ld][:, d - 1], dst_ids=[DstId(rid=rid, pnc=pid)],
                                            dma_engine_mask=(1 << e[2 * d - 2]) | (1 << e[2 * d - 1]), remote_sem=T.sem["ga%d" % t]))
            op("g", lambda: G.remote_dma_fused(tl, local_sem=T.sem["gl%d" % t]), [whole(gm)], [], ("gl%d" % t, 6))
            arrive(whole(ld), "ga%d" % t, 6)
        for k in (2, 3, 6, 7, 10):
            cp(r("XE", k, 4096, 16), r("XS"))
        cp(r("DNL"), r("K6", 0, 16))
        cp(r("CAN"), ind(r("CT"), r("DNL")))
        act(r("VF"), r("K3", 32, 48))
        for k in (11, 13, 14, 15):
            cp(r("XE", k, 4096, 16), r("XS"))

        def ecnt(n0, n1, bon, f):
            conv(f, "CM", n0, n1, r("K4", n0, n1), [(r(bon), r("EQS", n0, n1))])
        for j in range(2):
            act(r("GT", 512 * j, 512 * j + 512), ind(W, r("CAN", 32 * j, 32 * j + 32)))
        for j in range(3):
            n0 = 64 + 64 * j
            tt(r("CM", 16 * n0, 16 * n0 + 1024), ind(W, r("CAN", n0, n0 + 64)), r("XE", 16 * n0, 16 * n0 + 1024), O.is_lt)
            if j < 2:
                K = ("K1", "K2")[j]
                mm(r(K), [(r("ID"), r("XE", 512 * j, 512 * j + 512)), (r("IM1"), r("GT", 512 * j, 512 * j + 512))])
                act(r("CM", 512 * j, 512 * j + 512), r(K), F.Sign, bias=col(31))
            else:
                ecnt(0, 64, "B40", "HC")
            ecnt(n0, n0 + 64, "B32", "CNT")
        act(r("CS"), ind(r("CT"), r("DNL")), F.Identity, bias=col(9), scale=2.0 ** -16)
        if t == 0:
            consts(4)
        if more:
            for k in range(3):
                dma("y", rp("E", k, 2560, 3328), whole(ld, T[ld][:, :, k, :]))
        tt(r("COMB"), r("K4", 0, 256), r("CS"), O.add)
        tr(r("TR"), r("COMB"))
        scan(r("U"), r("MASK"), r("TR"), 0.0, O.mult, O.max)
        M = r("U", 15, 256, 16)
        ts(r("TT", 16, 32), M, r("TH", 2 * t, 2 * t + 1), None, O.is_lt)
        ts(r("MI"), M, 65536.0, None, O.mult)
        ts(r("VA"), M, 32.0, None, O.is_ge)
        ts(r("CI"), r("MI"), 4095, None, O.bitwise_and)
        tt(r("T1"), r("TT", 16, 32), r("NT"), O.mult)
        tt(r("TT", 32, 48), r("TT", 16, 32), r("VA"), O.mult)
        tt(r("TT", 0, 16), r("T1"), r("CI"), O.max)
        ttol("TT", 48, "K6", 64)
        ts(r("DQ", 0, 16), r("CI"), 15, None, O.bitwise_and)
        ts(r("DQ", 16, 32), r("CI"), 4, 15, O.arith_shift_right, O.bitwise_and)
        ts(r("DQ", 32, 48), r("CI"), 8, None, O.arith_shift_right)
        for k in range(3):
            cp(r("Q", k, 256, 16), r("DQ", 16 * k, 16 * k + 16))
        tr(r("EV"), r("Q"))
        cp(r("Lf"), r("K6", 64, 112))
        cp(r("RFB"), r("Lf", 32, 48))
        tt(r("E1t"), r("Lf", 16, 32), r("NLE"), O.mult)
        mm(r("K7", 16, 32), [(r("B16"), r("RFB"))])
        mm(r("K7", 0, 16), [(r("LT"), r("RFB")), (r("IM1K"), r("RFB"))])
        tt(r("PE_"), r("E1t"), r("VF"), O.max)
        dd1("Lf", 256, "RX")
        cp(r("POSE"), r("PE_"))

        def escat():
            cp(ind(r("E"), r("POSE")), r("EV"))
        if more:
            escat()
            for c0, c1 in VC:
                addend("E", c0, c1)
            conv("FF", "E", 0, 160, r("K0", 0, 160), [(r("I16"), r("N1H")), (r("ID"), r("ANb", 0, 160))])
        ms(r("GX", 0, 1), 1024.0)
        scan(r("GX", 1, 17), r("ON160", 0, 16), r("K7", 16, 32), 1024.0, O.mult, O.add)
        ms(r("NG", 0, 64), 0.0)
        tt(r("RR"), r("K7", 0, 16), r("GX", 0, 16), O.add)
        ts(r("BAD"), r("RR"), 63.5, None, O.is_gt)
        ts(r("RM"), r("RR"), 63.0, None, O.min)
        tt(r("BAD"), r("BAD"), r("G64"), O.mult)
        tt(r("GP"), r("BAD"), r("RM"), O.max)
        cp(r("POSG"), r("GP"))
        cp(ind(r("NG"), r("POSG")), r("N1b"))
        conv("CNT", "NG", 0, 4, r("K7", 32, 36))
        if more:
            mm(r("K6", 0, 16), [(r("ONEf"), r("TT", 16, 32))])
        ts(r("NL", 0, 4), r("K7", 32, 36), 0.0625, -1.0, O.mult, O.add)
        ts(r("INV", 0, 4), r("K7", 32, 36), 0.5, 8192.0, O.is_lt, O.mult)
        gs = "GS%d" % t
        act(r("GH"), ind(r("DGH"), r("NL", 0, 4)))
        act(r("GLo"), ind(r("DGL"), r("NL", 0, 4)))
        act(r(gs, 0, 64), ind(r("XS"), r("NL", 0, 4)))
        conv("CNT", "GH", 0, 4, r("K7", 36, 40))
        conv("CNT", "GLo", 0, 4, r("K7", 40, 44))
        if more:
            cp(r("P1L"), r("K0", 0, 160))
        dd2("Lf", 256, "CRU", "EQ")
        tt(r("INV", 4, 8), r("K7", 36, 40), r("INV", 0, 4), O.add)
        ts(r(gs, 64, 68), r("INV", 4, 8), 4096.0, None, O.min)
        cp(r(gs, 68, 72), r("K7", 40, 44))
        dst = T.cores[(rank + 1 + t % 3) % N]
        rid, pid, _ = topo.addr(dst)
        mask = sum(1 << e for e in topo.engines(core, dst)[:8])
        op("g", lambda: G.remote_dma(out_ap=T["GR%d" % t][:], in_ap=T[gs][:], remote_sem=T.sem["ua%d" % t], local_sem=T.sem["ul%d" % t],
                                     pid=pid, routing_id=rid, dma_engine_mask=mask), [r(gs)], [], ("ul%d" % t, 8))
        if more:
            act(r("E1", 2560, 3328), r("E", 2560, 3328))
            act(r("E2", 2560, 3328), r("E", 2560, 3328))
            red(r("HS", 0, 1), r("K6", 0, 16))
            cp(r("HI", 0, 1), r("HS", 0, 1))
            ts(r("HI", 1, 2), r("HI", 0, 1), 1, None, O.bitwise_and)
            ts(r("TH", 2 * t + 2, 2 * t + 3), r("HI", 1, 2), 41.0, None, O.add)
            ts(r("TH", 2 * t + 3, 2 * t + 4), r("HI", 1, 2), 9.0, None, O.add)
        dd3(256, "WIN")
    escat()
    sel(15, [(8, 1), (9, 16), (10, 256)])
    dd4("Lf", 256, "POSS", r("XS"))
    ts(r("YT"), r("CNT", 128, 256), col(15), None, O.mult)
    tt(r("YW"), r("FD", 0, 128), r("YT"), O.add)
    guest1(RO - 1)
    guest2(RO - 1)
    for c in range(5):
        K = ("K0", "K1")[c % 2]
        mm(r(K), [(r("YW"), r("E", 512 * c, 512 * c + 512))])
        act(r("OUT", 512 * c, 512 * c + 512), r(K))
    dma("y", whole("yof"), rp("OUT", 0, 0, 2560))
    dma("y", whole("yan"), rp("OUT", 1, 0, 2560))
    guest3(RO - 1)
    guest4(RO - 1)
    dd2("Lg", 64, "CRUg", "EQg")
    dd3(64, "WINg")
    dd4("Lg", 64, "POSQ", r("GR%d" % (RO - 1), 0, 64))
    dma("y", whole("ys"), r("S", 0, 4096))
    for c in sorted(cnt):
        if known["g"].get(c, 0) < cnt[c]:
            G.wait_ge(T.sem[c], cnt[c])
